import numpy as np
import ml_dtypes


def mxq(x, axis, fmt="e4m3"):
    dtype, down = {"e4m3": (ml_dtypes.float8_e4m3fn, 7), "e5m2": (ml_dtypes.float8_e5m2, 14)}[fmt]
    v = np.moveaxis(np.asarray(x, np.float32).astype(ml_dtypes.bfloat16).astype(np.float64), axis, -1)
    blocks = v.reshape(v.shape[:-1] + (-1, 32))
    amax = np.abs(blocks).max(-1, keepdims=True)
    byte = np.maximum(np.where(amax > 0, np.frexp(amax)[1] - 1 + 127, 0) - down, 1)
    scale = np.exp2(byte - 127.0)
    codes = (blocks / scale).astype(np.float32).astype(dtype).astype(np.float64)
    return np.moveaxis((codes * scale).reshape(v.shape), -1, axis)


WIDE = False


def mx_kscale(k):
    if not WIDE:
        return np.ones(k)
    levels = np.array([10, -10, 5, -5, 0])
    if k % 512:
        return np.exp2(np.random.permutation(np.resize(levels, k // 32))).repeat(32)
    a = np.empty((k // 512, 16))
    for p in range(k // 512):
        a[p, :8] = np.random.permutation(np.resize(levels, 8))
        for g in range(8):
            far = levels[np.abs(levels - a[p, g]) >= 10]
            a[p, g + 8] = far[np.random.randint(len(far))]
    return np.exp2(a.ravel()).repeat(32)


def f64(x):
    return np.asarray(x).astype(np.float64)


def striped(idx):
    return np.tile(np.asarray(idx).reshape(-1, 16).T, (8, 1)).astype(np.uint16)


def unstriped(offs):
    return offs[:16].T.reshape(-1).astype(np.int64)


E2M1 = np.array([0.0, 0.5, 1.0, 1.5, 2.0, 3.0, 4.0, 6.0, -0.0, -0.5, -1.0, -1.5, -2.0, -3.0, -4.0, -6.0])


def pack_weight(w, fmt):
    k, n = w.shape
    w = f64(np.asarray(w, np.float32).astype(ml_dtypes.bfloat16)).reshape(k // 32, 32, n)
    amax = np.abs(w).max(1)
    if fmt == "e4m3":
        byte = np.frexp(amax)[1] - 1 + 127 - 7
    else:
        mant, ex = np.frexp(amax / 6.0)
        byte = np.where(mant > 0.5, ex, ex - 1) + 127
    byte = np.clip(np.where(amax > 0, byte, 1), 1, 254)
    scaled = (w * np.exp2(127.0 - byte)[:, None, :]).reshape(k, n).astype(np.float32)
    by_word = np.ascontiguousarray(scaled.reshape(k // 512, 128, 4, n).transpose(0, 1, 3, 2))
    if fmt == "e4m3":
        words = by_word.astype(ml_dtypes.float8_e4m3fn).view(np.uint8)
    else:
        c = by_word.astype(ml_dtypes.float4_e2m1fn).view(np.uint8) & 0xF
        words = (c[..., 0::2] | (c[..., 1::2] << 4)).reshape(k // 512, 128, 2 * n)
    return np.ascontiguousarray(words), np.ascontiguousarray(byte.astype(np.uint8).reshape(k // 512, 16, n))


def unpack_weight(words, scales, fmt):
    g, _, n = scales.shape
    words = np.ascontiguousarray(words).reshape(g, 128, n, -1)
    if fmt == "e4m3":
        vals = words.view(ml_dtypes.float8_e4m3fn).astype(np.float64)
    else:
        nib = np.empty((g, 128, n, 4), np.uint8)
        nib[..., 0::2] = words & 0xF
        nib[..., 1::2] = words >> 4
        vals = E2M1[nib]
    vals = vals * np.repeat(np.exp2(scales.astype(np.float64) - 127.0), 8, axis=1)[..., None]
    return vals.transpose(0, 1, 3, 2).reshape(g * 512, n)


def bf(x):
    return np.asarray(x, np.float32).astype(ml_dtypes.bfloat16)


def planes(Y):
    r, m = Y.shape
    b = f64(bf(Y)).reshape(r // 32, 32, m)
    amax = np.abs(b).max(1)
    byte = np.clip(np.where(amax > 0, np.frexp(amax)[1] - 1 + 127 - 7, 1), 1, 254)
    codes = (b * np.exp2(127.0 - byte)[:, None, :]).reshape(r, m).astype(np.float32).astype(ml_dtypes.float8_e4m3fn).view(np.uint8)
    words = codes.reshape(r // 512, 128, 4, m).transpose(0, 1, 3, 2)
    return np.ascontiguousarray(words), np.ascontiguousarray(byte.astype(np.uint8).reshape(r // 512, 16, m))


D, T, I, Q, E, V, M = 512, 2048, 512, 256, 512, 32, 1024


def setup_inputs():
    n = np.random.standard_normal
    idx = np.random.permutation(T)[:I]
    idx2 = np.random.permutation(M)[:Q]
    idx4 = np.random.permutation(I)[:I]
    fd = mx_kscale(D)
    fi = mx_kscale(I)
    ti = np.ones(T)
    ti[idx] = fi
    keysp = pack_weight(n((D, T)) / fd[:, None], "e2m1")
    return {
        "query": (n((D, Q)) * 1.0 / np.sqrt(D) * fd[:, None]).astype(np.float32),
        "keys_words": keysp[0],
        "keys_scales": keysp[1],
        "lam": (np.random.uniform(0.3, 0.8, (1, Q))).astype(np.float32),
        "rival": (np.random.uniform(0.5, 2.0, (Q, 1))).astype(np.float32),
        "os": (np.random.uniform(4.0, 16.0, (1, I)) * fi).astype(np.float32),
        "vals": (n((E, T)) / ti).astype(np.float32),
        "member": (n((E, M))).astype(np.float32),
        "mgain": np.tile(np.random.uniform(0.5, 2.0, M), (128, 1)).astype(np.float32),
        "offs": striped(idx),
        "offs2": striped(idx2),
        "offs4": striped(idx4),
    }


def reference(query, keys_words, keys_scales, lam, rival, os, vals, member, mgain, offs, offs2, offs4):
    idx = unstriped(offs)
    idx2 = unstriped(offs2)
    idx4 = unstriped(offs4)
    keysu = unpack_weight(keys_words, keys_scales, "e2m1")
    keysidxg = keysu[:, idx]
    queryq = mxq(f64(query), 0, "e4m3")
    a0 = keysidxg.T @ queryq
    ag = a0.reshape(I, V, Q // V).max(axis=2)
    ar = np.repeat(ag, Q // V, axis=1)
    s0 = a0 - ar * f64(lam)
    s = s0.T
    p = np.exp(s)
    r = p / (p + p[:, idx4] * f64(rival))
    w = r / np.sum(r, axis=1, keepdims=True)
    wo1 = w * f64(os)
    wt1 = wo1.T
    vt1 = f64(vals)[:, idx].T
    vt1q = mxq(vt1, 0, "e4m3")
    wt1q = mxq(wt1, 0, "e4m3")
    o = vt1q.T @ wt1q
    y = o * f64(mgain)[:1][:, idx2] + f64(member)[:, idx2]
    words, scales = planes(y)
    return y, words, scales

@@ -1,0 +1,322 @@
+from contextlib import ExitStack
+
+import concourse.mybir as mybir
+from concourse.masks import make_identity
+
+D, T, I, Q, E, M = 512, 2048, 512, 256, 512, 1024
+GROUP = 8
+FLOPS = 2 * D * I * Q + 2 * I * E * Q
+
+F32 = mybir.dt.float32
+BF16 = mybir.dt.bfloat16
+I32 = mybir.dt.int32
+U32 = mybir.dt.uint32
+U16 = mybir.dt.uint16
+U8 = mybir.dt.uint8
+FP8X4 = mybir.dt.float8_e4m3fn_x4
+FP4X4 = mybir.dt.float4_e2m1fn_x4
+ACT = mybir.ActivationFunctionType
+ALU = mybir.AluOpType
+AXIS = mybir.AxisListType
+
+P = 128
+PACK = 4
+HALVES = Q // P
+
+
+def tile_attend_groupbest_overlinked_bymember_pl_kernel(
+    tc, query, keys_words, keys_scales, lam, rival, slot_factor, vals, member, mgain, offs, offs2, offs4, out_0, out_1, out_2
+):
+    nc = tc.nc
+    with ExitStack() as ctx:
+        sb = ctx.enter_context(tc.tile_pool(name="sb", bufs=1))
+        ps = ctx.enter_context(tc.psum_pool(name="ps", bufs=1))
+
+        def tile(shape, dtype, name, tag=None):
+            return sb.tile(shape, dtype, name=name, tag=tag or name, align_bytes=64)
+
+        slot_list = sb.tile([P, I // 16], U16, name="slot_list")
+        member_list = sb.tile([P, Q // 16], U16, name="member_list")
+        rival_list = sb.tile([P, I // 16], U16, name="rival_list")
+        key_words = tile([P, T], U16, "key_words")
+        key_scales = tile([P, T], U8, "key_scales")
+        q_raw = tile([P, PACK, Q], F32, "q_raw")
+        lam_col = tile([P, HALVES], F32, "lam_col")
+        rival_col = tile([P, HALVES], F32, "rival_col")
+        os_col = tile([P, PACK], F32, "os_col")
+        gain_pool = tile([P, M], F32, "gain_pool")
+        val_pool = [tile([P, T], F32, f"val_pool{j}") for j in range(PACK)]
+        mem_pool = [tile([P, M], F32, f"mem_pool{j}") for j in range(PACK)]
+        ident = tile([P, P], F32, "ident")
+
+        nc.vector.memset(key_scales[:].bitcast(I32), 0)
+        nc.sync.dma_start(slot_list[:], offs)
+        nc.sync.dma_start(q_raw[:], query.rearrange("(p j) q -> p j q", j=PACK))
+        with nc.allow_non_contiguous_dma(reason="one value to a partition"):
+            nc.sync.dma_start(lam_col[:], lam.rearrange("o (h p) -> p (o h)", p=P))
+        for quad in range(4):
+            nc.sync.dma_start(
+                key_scales[32 * quad : 32 * quad + 4, :].bitcast(I32),
+                keys_scales[0, 4 * quad : 4 * quad + 4, :].bitcast(I32),
+            )
+        nc.sync.dma_start(key_words[:].bitcast(I32), keys_words[0].bitcast(I32))
+        make_identity(nc, ident[:])
+        nc.gpsimd.memset(gain_pool[:], 0.0)
+        vals_dealt = vals.rearrange("(p j) t -> j p t", j=PACK)
+        member_dealt = member.rearrange("(p j) m -> j p m", j=PACK)
+        nc.sync.dma_start(member_list[:], offs2)
+        nc.sync.dma_start(gain_pool[0:1, :], mgain[0:1, :])
+        nc.sync.dma_start(mem_pool[0][:], member_dealt[0])
+        nc.sync.dma_start(val_pool[0][:], vals_dealt[0])
+        nc.sync.dma_start(rival_list[:], offs4)
+        nc.sync.dma_start(val_pool[1][:], vals_dealt[1])
+        with nc.allow_non_contiguous_dma(reason="one value to a partition"):
+            nc.sync.dma_start(rival_col[:], rival.rearrange("(h p) o -> p (h o)", p=P))
+        nc.sync.dma_start(os_col[:], slot_factor.rearrange("o (p t) -> p (o t)", t=PACK))
+        nc.sync.dma_start(val_pool[2][:], vals_dealt[2])
+        nc.sync.dma_start(val_pool[3][:], vals_dealt[3])
+        nc.sync.dma_start(mem_pool[1][:], member_dealt[1])
+        nc.sync.dma_start(mem_pool[2][:], member_dealt[2])
+        nc.sync.dma_start(mem_pool[3][:], member_dealt[3])
+
+        k_words = [tile([P, 2 * P], U16, f"k_words{b}") for b in range(2)]
+        k_scales = tile([P, I], U8, "k_scales")
+        q_bf = tile([P, Q, PACK], BF16, "q_bf")
+        q_codes = tile([P, Q], U32, "q_codes")
+        q_scales = tile([P, Q], U8, "q_scales")
+
+        q_src = q_raw[:].rearrange("p t (c i) -> p c t i", i=4)
+        q_dst = q_bf[:].rearrange("p (c i) t -> p c t i", i=4)
+        split = 48
+        nc.scalar.activation(q_dst[:, :split], q_src[:, :split], ACT.Copy)
+        nc.vector.tensor_copy(q_dst[:, split:], q_src[:, split:])
+        nc.vector.quantize_mx(q_codes[:].bitcast(FP8X4), q_scales[:], q_bf[:].rearrange("p c t -> p (c t)"))
+        nc.vector.tensor_copy(k_scales[:], key_scales[:].indirect(slot_list[:]))
+        for b in range(2):
+            nc.vector.tensor_copy(k_words[b][:], key_words[:].indirect(slot_list[:, 16 * b : 16 * (b + 1)]))
+
+        rows = ps.tile([P, 2 * Q], F32, name="rows", tag="rows")
+        for h in range(HALVES):
+            nc.tensor.transpose(rows[:, h * P : (h + 1) * P], lam_col[:, h : h + 1].to_broadcast([P, P]), ident[:])
+
+        raw = [ps.tile([P, 2, Q], F32, name=f"raw{b}", tag=f"product{b}") for b in range(2)]
+        for b in range(2):
+            for c in range(2):
+                block = 2 * b + c
+                nc.tensor.matmul_mx(
+                    raw[b][:, c, :],
+                    lhsT=k_words[b][:, c * P : (c + 1) * P].bitcast(FP4X4),
+                    lhsT_scale=k_scales[:, block * P : (block + 1) * P],
+                    rhs=q_codes[:].bitcast(FP8X4),
+                    rhs_scale=q_scales[:],
+                    start=True,
+                    stop=True,
+                )
+
+        groups = Q // GROUP
+        lam_rows = rows[:, 0:Q].rearrange("p (o v g) -> p o v g", o=1, g=GROUP).to_broadcast([P, 2, groups, GROUP])
+        raw_sb = [tile([P, 2, Q], F32, f"raw_sb{b}") for b in range(2)]
+        shift = [tile([P, 2, groups, GROUP], F32, f"shift{b}") for b in range(2)]
+        neg_best = [tile([P, 2, groups, 1], F32, f"neg_best{b}") for b in range(2)]
+
+        def group_best(b):
+            nc.vector.tensor_reduce(
+                neg_best[b][:].rearrange("p c v o -> p (c v o)"),
+                raw[b][:].rearrange("p c (v g) -> p (c v) g", g=GROUP),
+                axis=AXIS.X,
+                op=ALU.max,
+                negate=True,
+            )
+
+        def group_shift(b):
+            nc.vector.tensor_tensor(
+                shift[b][:], neg_best[b][:].to_broadcast([P, 2, groups, GROUP]), lam_rows, ALU.mult
+            )
+
+        group_best(0)
+        nc.scalar.copy(raw_sb[0][:], raw[0][:])
+        group_best(1)
+        nc.scalar.copy(raw_sb[1][:], raw[1][:])
+        group_shift(0)
+        group_shift(1)
+
+        score = [ps.tile([P, I], F32, name=f"score{h}", tag=f"turn{h}") for h in range(HALVES)]
+        shift_flat = [s[:].rearrange("p c v g -> p c (v g)") for s in shift]
+        terms = [(0, raw_sb[0][:]), (0, shift_flat[0]), (1, raw_sb[1][:]), (1, shift_flat[1])]
+        for h in range(HALVES):
+            for n, (b, term) in enumerate(terms):
+                for c in range(2):
+                    block = 2 * b + c
+                    nc.tensor.matmul(
+                        score[h][:, block * P : (block + 1) * P],
+                        lhsT=term[:, c, h * P : (h + 1) * P],
+                        rhs=ident[:],
+                        is_transpose=True,
+                        start=(n == 0 and c == 0),
+                        stop=(n == len(terms) - 1 and c == 1),
+                    )
+
+        gain_row = tile([P, Q], F32, "gain_row", None)
+        gain_col = tile([P, HALVES], F32, "gain_col")
+        gain = tile([P, Q], F32, "gain")
+        nc.scalar.activation(gain_row[:], gain_pool[:].indirect(member_list[:]), ACT.Copy)
+        gain_turned = ps.tile([P, HALVES, P], F32, name="gain_turned", tag="values1")
+        for h in range(HALVES):
+            nc.tensor.transpose(gain_turned[:, h, :], gain_row[:, h * P : (h + 1) * P], ident[:])
+        nc.scalar.copy(gain_col[:], gain_turned[:, :, 0])
+        gain_spread = ps.tile([P, Q], F32, name="gain_spread", tag="values1")
+        for h in range(HALVES):
+            nc.tensor.transpose(
+                gain_spread[:, h * P : (h + 1) * P], gain_col[:, h : h + 1].to_broadcast([P, P]), ident[:]
+            )
+        nc.scalar.copy(gain[:], gain_spread[:])
+
+        v_codes = [tile([P, 2 * P], U32, f"v_codes{r}") for r in range(2)]
+        v_scales = [tile([P, 2 * P], U8, f"v_scales{r}") for r in range(2)]
+        v_turned = [ps.tile([P, 2, 2, P], F32, name=f"v_turned{r}", tag=f"values{r}") for r in range(2)]
+
+        def turn(picked, turned):
+            pairs = picked.bitcast(F32)
+            for u in range(2):
+                nc.tensor.transpose(turned[:, u, :], pairs[:, u : I // 2 : 2], ident[:])
+
+        def gather_values(j, on_scalar):
+            picked = tile([P, I], BF16, f"v_picked{j}", ["q_codes",None,"p_inv1",None][j])
+            if on_scalar:
+                nc.scalar.activation(picked[:], val_pool[j][:].indirect(slot_list[:]), ACT.Copy)
+            else:
+                nc.vector.tensor_copy(picked[:], val_pool[j][:].indirect(slot_list[:]))
+            turn(picked[:], v_turned[j // 2][:, j % 2])
+
+        def quantize_values(r, copy):
+            grouped = tile([P, 2 * P * PACK], BF16, f"v_grouped{r}", ["root0",None][r])
+            copy(
+                grouped[:].bitcast(F32).rearrange("p (j c u) -> p j c u", j=2, u=2),
+                v_turned[r][:].rearrange("p j u c -> p j c u"),
+            )
+            nc.vector.quantize_mx(v_codes[r][:].bitcast(FP8X4), v_scales[r][:], grouped[:])
+
+        p_sb = [tile([P, I], F32, f"p{h}") for h in range(HALVES)]
+        p_inv = [tile([P, I], F32, f"p_inv{h}") for h in range(HALVES)]
+        ratio = [tile([P, I], F32, f"ratio{h}") for h in range(HALVES)]
+        for h in range(HALVES):
+            nc.scalar.activation(p_sb[h][:], score[h][:], ACT.Exp)
+            nc.scalar.activation(p_inv[h][:], score[h][:], ACT.Exp, scale=-1.0)
+        for h in range(HALVES):
+            for c in range(2):
+                cols = slice(c * I // 2, (c + 1) * I // 2)
+                nc.vector.tensor_tensor(
+                    ratio[h][:, cols],
+                    p_sb[h][:].indirect(rival_list[:, 16 * c : 16 * (c + 1)]),
+                    p_inv[h][:, cols],
+                    ALU.mult,
+                )
+
+        os_rows = ps.tile([P, PACK, P], F32, name="os_rows", tag="os_rows")
+        for t in range(PACK):
+            nc.tensor.transpose(os_rows[:, t, :], os_col[:, t : t + 1].to_broadcast([P, P]), ident[:])
+
+        root = [tile([P, I], F32, f"root{h}") for h in range(HALVES)]
+        part = [tile([P, I], F32, f"part{h}") for h in range(HALVES)]
+        part_sum = [tile([P, 1], F32, f"part_sum{h}") for h in range(HALVES)]
+        inv_sum = [tile([P, 1], F32, f"inv_sum{h}") for h in range(HALVES)]
+        w_bf = [tile([P, I], BF16, f"w_bf{h}") for h in range(HALVES)]
+        w_codes = [tile([P, P], U32, f"w_codes{h}") for h in range(HALVES)]
+        w_scales = [tile([P, P], U8, f"w_scales{h}") for h in range(HALVES)]
+
+        def inverse_root(h):
+            nc.scalar.activation(
+                root[h][:], ratio[h][:], ACT.Abs_reciprocal_sqrt, scale=rival_col[:, h : h + 1], bias=1.0
+            )
+
+        def square(h, on_scalar):
+            if on_scalar:
+                nc.scalar.activation(part[h][:], root[h][:], ACT.Square, accum_out=part_sum[h][:])
+            else:
+                nc.vector.scalar_tensor_tensor(
+                    part[h][:], root[h][:], 1.0, root[h][:], ALU.mult, ALU.mult, accum_out=part_sum[h][:]
+                )
+
+        inverse_root(0)
+        inverse_root(1)
+        square(0, True)
+        square(1, True)
+        for h in range(HALVES):
+            nc.vector.reciprocal(inv_sum[h][:], part_sum[h][:])
+            nc.vector.scalar_tensor_tensor(
+                w_bf[h][:].rearrange("q (p t) -> q p t", t=PACK),
+                part[h][:].rearrange("q (p t) -> q p t", t=PACK),
+                inv_sum[h][:],
+                os_rows[:].rearrange("q t p -> q p t"),
+                ALU.mult,
+                ALU.mult,
+            )
+            w_turned = ps.tile([P, 2, P], F32, name=f"w_turned{h}", tag=f"turn{h}")
+            turn(w_bf[h][:], w_turned)
+            w_grouped = tile([P, P * PACK], BF16, f"w_grouped{h}")
+            nc.scalar.copy(
+                w_grouped[:].bitcast(F32).rearrange("p (c u) -> p c u", u=2), w_turned[:].rearrange("p u c -> p c u")
+            )
+            nc.vector.quantize_mx(w_codes[h][:].bitcast(FP8X4), w_scales[h][:], w_grouped[:])
+
+        gather_values(0, True)
+        gather_values(1, False)
+        quantize_values(0, nc.scalar.copy)
+        gather_values(2, False)
+        gather_values(3, False)
+        quantize_values(1, nc.scalar.copy)
+
+        dense = 3
+        runs = [[0,1,None],[1,3,None]]
+        mem_picked = [tile([P, hi - lo, Q], F32, f"mem_picked{lo}", hold) for lo, hi, hold in runs]
+        for (lo, hi, hold), picked in zip(runs, mem_picked):
+            for j in range(lo, hi):
+                nc.scalar.activation(picked[:, j - lo, :], mem_pool[j][:].indirect(member_list[:]), ACT.Copy)
+        scaled = [tile([P, PACK, P], F32, f"scaled{h}") for h in range(HALVES)]
+        y = tile([P, PACK, Q], F32, "y")
+        y_bf = [tile([P, P, PACK], BF16, f"y_bf{h}") for h in range(HALVES)]
+        y_codes = tile([P, Q], U32, "y_codes")
+        y_scales = tile([P, Q], U8, "y_scales")
+        out_dealt = out_0.rearrange("(p j) q -> p j q", j=PACK)
+        for h in range(HALVES):
+            cols = slice(h * P, (h + 1) * P)
+            o = ps.tile([P, PACK, P], F32, name=f"o{h}", tag=f"product{h}")
+            for j in range(PACK):
+                e_cols = slice((j % 2) * P, (j % 2 + 1) * P)
+                nc.tensor.matmul_mx(
+                    o[:, j, :],
+                    lhsT=v_codes[j // 2][:, e_cols].bitcast(FP8X4),
+                    lhsT_scale=v_scales[j // 2][:, e_cols],
+                    rhs=w_codes[h][:].bitcast(FP8X4),
+                    rhs_scale=w_scales[h][:],
+                    start=True,
+                    stop=True,
+                )
+            nc.vector.tensor_tensor(
+                scaled[h][:],
+                o[:],
+                gain[:, cols].rearrange("p (o c) -> p o c", o=1).to_broadcast([P, PACK, P]),
+                ALU.mult,
+            )
+            for (lo, hi, hold), picked in zip(runs, mem_picked):
+                nc.vector.tensor_tensor(y[:, lo:hi, cols], picked[:, :, cols], scaled[h][:, lo:hi, :], ALU.add)
+            for j in range(dense, PACK):
+                if True:
+                    addend = mem_pool[j][:].indirect(member_list[:, 8 * h : 8 * (h + 1)])
+                    nc.vector.tensor_tensor(y[:, j, cols], addend, scaled[h][:, j, :], ALU.add)
+            nc.sync.dma_start(out_dealt[:, :, cols], y[:, :, cols])
+            src = y[:, :, cols].rearrange("p t (c i) -> p c t i", i=4)
+            dst = y_bf[h][:].rearrange("p (c i) t -> p c t i", i=4)
+            [nc.scalar.copy, nc.vector.tensor_copy][h](dst, src)
+        nc.vector.quantize_mx(
+            y_codes[:, :P].bitcast(FP8X4), y_scales[:, :P], y_bf[0][:].rearrange("p c t -> p (c t)")
+        )
+        nc.vector.quantize_mx(
+            y_codes[:, P:].bitcast(FP8X4), y_scales[:, P:], y_bf[1][:].rearrange("p c t -> p (c t)")
+        )
+        nc.sync.dma_start(out_1[0].rearrange("p c r -> p (c r)").bitcast(I32), y_codes[:].bitcast(I32))
+        for quad in range(4):
+            nc.scalar.dma_start(
+                out_2[0, 4 * quad : 4 * quad + 4, :].bitcast(I32),
+                y_scales[32 * quad : 32 * quad + 4, :].bitcast(I32),
+            )

@@ -22,62 +22,63 @@ AXIS = mybir.AxisListType
 P = 128
 PACK = 4
 HALVES = Q // P
+GROUPS = Q // GROUP
+LIST_ROWS = 16
 
 
 def tile_attend_groupbest_overlinked_bymember_pl_kernel(
-    tc, query, keys_words, keys_scales, lam, rival, slot_factor, vals, member, mgain, offs, offs2, offs4, out_0, out_1, out_2
+    tc, query, keys_words, keys_scales, lam, rival, slot_factor, vals, member, mgain, offs, offs2, offs4,
+    out_0, out_1, out_2,
 ):
     nc = tc.nc
     with ExitStack() as ctx:
         sb = ctx.enter_context(tc.tile_pool(name="sb", bufs=1))
         ps = ctx.enter_context(tc.psum_pool(name="ps", bufs=1))
 
-        def tile(shape, dtype, name, tag=None):
-            return sb.tile(shape, dtype, name=name, tag=tag or name, align_bytes=64)
+        def tile(shape, dtype, name, reuse=None):
+            return sb.tile(shape, dtype, name=name, tag=reuse or name, align_bytes=64)
 
-        slot_list = sb.tile([P, I // 16], U16, name="slot_list")
-        member_list = sb.tile([P, Q // 16], U16, name="member_list")
-        rival_list = sb.tile([P, I // 16], U16, name="rival_list")
+        slot_list = sb.tile([P, I // LIST_ROWS], U16, name="slot_list")
+        member_list = sb.tile([P, Q // LIST_ROWS], U16, name="member_list")
+        rival_list = sb.tile([P, I // LIST_ROWS], U16, name="rival_list")
         key_words = tile([P, T], U16, "key_words")
         key_scales = tile([P, T], U8, "key_scales")
         q_raw = tile([P, PACK, Q], F32, "q_raw")
         lam_col = tile([P, HALVES], F32, "lam_col")
         rival_col = tile([P, HALVES], F32, "rival_col")
-        os_col = tile([P, PACK], F32, "os_col")
+        factor_col = tile([P, PACK], F32, "factor_col")
         gain_pool = tile([P, M], F32, "gain_pool")
         val_pool = [tile([P, T], F32, f"val_pool{j}") for j in range(PACK)]
         mem_pool = [tile([P, M], F32, f"mem_pool{j}") for j in range(PACK)]
         ident = tile([P, P], F32, "ident")
+        vals_dealt = vals.rearrange("(p j) t -> j p t", j=PACK)
+        member_dealt = member.rearrange("(p j) m -> j p m", j=PACK)
 
         nc.vector.memset(key_scales[:].bitcast(I32), 0)
+        nc.vector.memset(gain_pool[:], 0.0)
+        make_identity(nc, ident[:])
         nc.sync.dma_start(slot_list[:], offs)
+        nc.sync.dma_start(key_words[:].bitcast(I32), keys_words[0].bitcast(I32))
         nc.sync.dma_start(q_raw[:], query.rearrange("(p j) q -> p j q", j=PACK))
-        with nc.allow_non_contiguous_dma(reason="one value to a partition"):
-            nc.sync.dma_start(lam_col[:], lam.rearrange("o (h p) -> p (o h)", p=P))
         for quad in range(4):
             nc.sync.dma_start(
                 key_scales[32 * quad : 32 * quad + 4, :].bitcast(I32),
                 keys_scales[0, 4 * quad : 4 * quad + 4, :].bitcast(I32),
             )
-        nc.sync.dma_start(key_words[:].bitcast(I32), keys_words[0].bitcast(I32))
-        make_identity(nc, ident[:])
-        nc.gpsimd.memset(gain_pool[:], 0.0)
-        vals_dealt = vals.rearrange("(p j) t -> j p t", j=PACK)
-        member_dealt = member.rearrange("(p j) m -> j p m", j=PACK)
+        with nc.allow_non_contiguous_dma(reason="one value to a partition"):
+            nc.sync.dma_start(lam_col[:], lam.rearrange("o (h p) -> p (o h)", p=P))
+        nc.sync.dma_start(val_pool[0][:], vals_dealt[0])
         nc.sync.dma_start(member_list[:], offs2)
         nc.sync.dma_start(gain_pool[0:1, :], mgain[0:1, :])
-        nc.sync.dma_start(mem_pool[0][:], member_dealt[0])
-        nc.sync.dma_start(val_pool[0][:], vals_dealt[0])
-        nc.sync.dma_start(rival_list[:], offs4)
         nc.sync.dma_start(val_pool[1][:], vals_dealt[1])
+        nc.sync.dma_start(rival_list[:], offs4)
+        nc.sync.dma_start(val_pool[2][:], vals_dealt[2])
         with nc.allow_non_contiguous_dma(reason="one value to a partition"):
             nc.sync.dma_start(rival_col[:], rival.rearrange("(h p) o -> p (h o)", p=P))
-        nc.sync.dma_start(os_col[:], slot_factor.rearrange("o (p t) -> p (o t)", t=PACK))
-        nc.sync.dma_start(val_pool[2][:], vals_dealt[2])
+        nc.sync.dma_start(factor_col[:], slot_factor.rearrange("o (p t) -> p (o t)", t=PACK))
         nc.sync.dma_start(val_pool[3][:], vals_dealt[3])
-        nc.sync.dma_start(mem_pool[1][:], member_dealt[1])
-        nc.sync.dma_start(mem_pool[2][:], member_dealt[2])
-        nc.sync.dma_start(mem_pool[3][:], member_dealt[3])
+        for j in range(PACK):
+            nc.sync.dma_start(mem_pool[j][:], member_dealt[j])
 
         k_words = [tile([P, 2 * P], U16, f"k_words{b}") for b in range(2)]
         k_scales = tile([P, I], U8, "k_scales")
@@ -85,19 +86,19 @@ def tile_attend_groupbest_overlinked_bymember_pl_kernel(
         q_codes = tile([P, Q], U32, "q_codes")
         q_scales = tile([P, Q], U8, "q_scales")
 
-        q_src = q_raw[:].rearrange("p t (c i) -> p c t i", i=4)
-        q_dst = q_bf[:].rearrange("p (c i) t -> p c t i", i=4)
-        split = 48
-        nc.scalar.activation(q_dst[:, :split], q_src[:, :split], ACT.Copy)
-        nc.vector.tensor_copy(q_dst[:, split:], q_src[:, split:])
+        nc.scalar.activation(
+            q_bf[:].rearrange("p (c i) t -> p c t i", i=4), q_raw[:].rearrange("p t (c i) -> p c t i", i=4), ACT.Copy
+        )
         nc.vector.quantize_mx(q_codes[:].bitcast(FP8X4), q_scales[:], q_bf[:].rearrange("p c t -> p (c t)"))
         nc.vector.tensor_copy(k_scales[:], key_scales[:].indirect(slot_list[:]))
         for b in range(2):
             nc.vector.tensor_copy(k_words[b][:], key_words[:].indirect(slot_list[:, 16 * b : 16 * (b + 1)]))
 
-        rows = ps.tile([P, 2 * Q], F32, name="rows", tag="rows")
+        lam_turned = ps.tile([P, Q], F32, name="lam_turned", tag="rows")
         for h in range(HALVES):
-            nc.tensor.transpose(rows[:, h * P : (h + 1) * P], lam_col[:, h : h + 1].to_broadcast([P, P]), ident[:])
+            nc.tensor.transpose(
+                lam_turned[:, h * P : (h + 1) * P], lam_col[:, h : h + 1].to_broadcast([P, P]), ident[:]
+            )
 
         raw = [ps.tile([P, 2, Q], F32, name=f"raw{b}", tag=f"product{b}") for b in range(2)]
         for b in range(2):
@@ -113,13 +114,11 @@ def tile_attend_groupbest_overlinked_bymember_pl_kernel(
                     stop=True,
                 )
 
-        groups = Q // GROUP
-        lam_rows = rows[:, 0:Q].rearrange("p (o v g) -> p o v g", o=1, g=GROUP).to_broadcast([P, 2, groups, GROUP])
+        lam_rows = lam_turned[:].rearrange("p (o v g) -> p o v g", o=1, g=GROUP).to_broadcast([P, 2, GROUPS, GROUP])
         raw_sb = [tile([P, 2, Q], F32, f"raw_sb{b}") for b in range(2)]
-        shift = [tile([P, 2, groups, GROUP], F32, f"shift{b}") for b in range(2)]
-        neg_best = [tile([P, 2, groups, 1], F32, f"neg_best{b}") for b in range(2)]
-
-        def group_best(b):
+        shift = [tile([P, 2, GROUPS, GROUP], F32, f"shift{b}") for b in range(2)]
+        neg_best = [tile([P, 2, GROUPS, 1], F32, f"neg_best{b}") for b in range(2)]
+        for b in range(2):
             nc.vector.tensor_reduce(
                 neg_best[b][:].rearrange("p c v o -> p (c v o)"),
                 raw[b][:].rearrange("p c (v g) -> p (c v) g", g=GROUP),
@@ -127,74 +126,27 @@ def tile_attend_groupbest_overlinked_bymember_pl_kernel(
                 op=ALU.max,
                 negate=True,
             )
-
-        def group_shift(b):
+            nc.scalar.copy(raw_sb[b][:], raw[b][:])
+        for b in range(2):
             nc.vector.tensor_tensor(
-                shift[b][:], neg_best[b][:].to_broadcast([P, 2, groups, GROUP]), lam_rows, ALU.mult
+                shift[b][:], neg_best[b][:].to_broadcast([P, 2, GROUPS, GROUP]), lam_rows, ALU.mult
             )
-
-        group_best(0)
-        nc.scalar.copy(raw_sb[0][:], raw[0][:])
-        group_best(1)
-        nc.scalar.copy(raw_sb[1][:], raw[1][:])
-        group_shift(0)
-        group_shift(1)
 
         score = [ps.tile([P, I], F32, name=f"score{h}", tag=f"turn{h}") for h in range(HALVES)]
-        shift_flat = [s[:].rearrange("p c v g -> p c (v g)") for s in shift]
-        terms = [(0, raw_sb[0][:]), (0, shift_flat[0]), (1, raw_sb[1][:]), (1, shift_flat[1])]
         for h in range(HALVES):
-            for n, (b, term) in enumerate(terms):
-                for c in range(2):
-                    block = 2 * b + c
-                    nc.tensor.matmul(
-                        score[h][:, block * P : (block + 1) * P],
-                        lhsT=term[:, c, h * P : (h + 1) * P],
-                        rhs=ident[:],
-                        is_transpose=True,
-                        start=(n == 0 and c == 0),
-                        stop=(n == len(terms) - 1 and c == 1),
-                    )
-
-        gain_row = tile([P, Q], F32, "gain_row", None)
-        gain_col = tile([P, HALVES], F32, "gain_col")
-        gain = tile([P, Q], F32, "gain")
-        nc.scalar.activation(gain_row[:], gain_pool[:].indirect(member_list[:]), ACT.Copy)
-        gain_turned = ps.tile([P, HALVES, P], F32, name="gain_turned", tag="values1")
-        for h in range(HALVES):
-            nc.tensor.transpose(gain_turned[:, h, :], gain_row[:, h * P : (h + 1) * P], ident[:])
-        nc.scalar.copy(gain_col[:], gain_turned[:, :, 0])
-        gain_spread = ps.tile([P, Q], F32, name="gain_spread", tag="values1")
-        for h in range(HALVES):
-            nc.tensor.transpose(
-                gain_spread[:, h * P : (h + 1) * P], gain_col[:, h : h + 1].to_broadcast([P, P]), ident[:]
-            )
-        nc.scalar.copy(gain[:], gain_spread[:])
-
-        v_codes = [tile([P, 2 * P], U32, f"v_codes{r}") for r in range(2)]
-        v_scales = [tile([P, 2 * P], U8, f"v_scales{r}") for r in range(2)]
-        v_turned = [ps.tile([P, 2, 2, P], F32, name=f"v_turned{r}", tag=f"values{r}") for r in range(2)]
-
-        def turn(picked, turned):
-            pairs = picked.bitcast(F32)
-            for u in range(2):
-                nc.tensor.transpose(turned[:, u, :], pairs[:, u : I // 2 : 2], ident[:])
-
-        def gather_values(j, on_scalar):
-            picked = tile([P, I], BF16, f"v_picked{j}", ["q_codes",None,"p_inv1",None][j])
-            if on_scalar:
-                nc.scalar.activation(picked[:], val_pool[j][:].indirect(slot_list[:]), ACT.Copy)
-            else:
-                nc.vector.tensor_copy(picked[:], val_pool[j][:].indirect(slot_list[:]))
-            turn(picked[:], v_turned[j // 2][:, j % 2])
-
-        def quantize_values(r, copy):
-            grouped = tile([P, 2 * P * PACK], BF16, f"v_grouped{r}", ["root0",None][r])
-            copy(
-                grouped[:].bitcast(F32).rearrange("p (j c u) -> p j c u", j=2, u=2),
-                v_turned[r][:].rearrange("p j u c -> p j c u"),
-            )
-            nc.vector.quantize_mx(v_codes[r][:].bitcast(FP8X4), v_scales[r][:], grouped[:])
+            for b in range(2):
+                terms = [raw_sb[b][:], shift[b][:].rearrange("p c v g -> p c (v g)")]
+                for n, term in enumerate(terms):
+                    for c in range(2):
+                        block = 2 * b + c
+                        nc.tensor.matmul(
+                            score[h][:, block * P : (block + 1) * P],
+                            lhsT=term[:, c, h * P : (h + 1) * P],
+                            rhs=ident[:],
+                            is_transpose=True,
+                            start=(b == 0 and n == 0 and c == 0),
+                            stop=(b == 1 and n == 1 and c == 1),
+                        )
 
         p_sb = [tile([P, I], F32, f"p{h}") for h in range(HALVES)]
         p_inv = [tile([P, I], F32, f"p_inv{h}") for h in range(HALVES)]
@@ -212,68 +164,97 @@ def tile_attend_groupbest_overlinked_bymember_pl_kernel(
                     ALU.mult,
                 )
 
-        os_rows = ps.tile([P, PACK, P], F32, name="os_rows", tag="os_rows")
+        factor_rows = ps.tile([P, PACK, P], F32, name="factor_rows", tag="factor_rows")
         for t in range(PACK):
-            nc.tensor.transpose(os_rows[:, t, :], os_col[:, t : t + 1].to_broadcast([P, P]), ident[:])
+            nc.tensor.transpose(factor_rows[:, t, :], factor_col[:, t : t + 1].to_broadcast([P, P]), ident[:])
 
         root = [tile([P, I], F32, f"root{h}") for h in range(HALVES)]
         part = [tile([P, I], F32, f"part{h}") for h in range(HALVES)]
         part_sum = [tile([P, 1], F32, f"part_sum{h}") for h in range(HALVES)]
         inv_sum = [tile([P, 1], F32, f"inv_sum{h}") for h in range(HALVES)]
         w_bf = [tile([P, I], BF16, f"w_bf{h}") for h in range(HALVES)]
-        w_codes = [tile([P, P], U32, f"w_codes{h}") for h in range(HALVES)]
-        w_scales = [tile([P, P], U8, f"w_scales{h}") for h in range(HALVES)]
-
-        def inverse_root(h):
+        w_codes = tile([P, Q], U32, "w_codes")
+        w_scales = tile([P, Q], U8, "w_scales")
+        for h in range(HALVES):
             nc.scalar.activation(
                 root[h][:], ratio[h][:], ACT.Abs_reciprocal_sqrt, scale=rival_col[:, h : h + 1], bias=1.0
             )
-
-        def square(h, on_scalar):
-            if on_scalar:
-                nc.scalar.activation(part[h][:], root[h][:], ACT.Square, accum_out=part_sum[h][:])
-            else:
-                nc.vector.scalar_tensor_tensor(
-                    part[h][:], root[h][:], 1.0, root[h][:], ALU.mult, ALU.mult, accum_out=part_sum[h][:]
-                )
-
-        inverse_root(0)
-        inverse_root(1)
-        square(0, True)
-        square(1, True)
         for h in range(HALVES):
+            nc.scalar.activation(part[h][:], root[h][:], ACT.Square, accum_out=part_sum[h][:])
+
+        def turn_pairs(rows_bf, turned):
+            pairs = rows_bf.bitcast(F32)
+            for u in range(2):
+                nc.tensor.transpose(turned[:, u, :], pairs[:, u : I // 2 : 2], ident[:])
+
+        for h in range(HALVES):
+            cols = slice(h * P, (h + 1) * P)
             nc.vector.reciprocal(inv_sum[h][:], part_sum[h][:])
             nc.vector.scalar_tensor_tensor(
                 w_bf[h][:].rearrange("q (p t) -> q p t", t=PACK),
                 part[h][:].rearrange("q (p t) -> q p t", t=PACK),
                 inv_sum[h][:],
-                os_rows[:].rearrange("q t p -> q p t"),
+                factor_rows[:].rearrange("q t p -> q p t"),
                 ALU.mult,
                 ALU.mult,
             )
             w_turned = ps.tile([P, 2, P], F32, name=f"w_turned{h}", tag=f"turn{h}")
-            turn(w_bf[h][:], w_turned)
+            turn_pairs(w_bf[h][:], w_turned)
             w_grouped = tile([P, P * PACK], BF16, f"w_grouped{h}")
-            nc.scalar.copy(
+            nc.vector.tensor_copy(
                 w_grouped[:].bitcast(F32).rearrange("p (c u) -> p c u", u=2), w_turned[:].rearrange("p u c -> p c u")
             )
-            nc.vector.quantize_mx(w_codes[h][:].bitcast(FP8X4), w_scales[h][:], w_grouped[:])
+            nc.vector.quantize_mx(w_codes[:, cols].bitcast(FP8X4), w_scales[:, cols], w_grouped[:])
 
-        gather_values(0, True)
-        gather_values(1, False)
-        quantize_values(0, nc.scalar.copy)
-        gather_values(2, False)
-        gather_values(3, False)
-        quantize_values(1, nc.scalar.copy)
+        v_codes = tile([P, E], U32, "v_codes")
+        v_scales = tile([P, E], U8, "v_scales")
 
-        dense = 3
-        runs = [[0,1,None],[1,3,None]]
-        mem_picked = [tile([P, hi - lo, Q], F32, f"mem_picked{lo}", hold) for lo, hi, hold in runs]
-        for (lo, hi, hold), picked in zip(runs, mem_picked):
-            for j in range(lo, hi):
-                nc.scalar.activation(picked[:, j - lo, :], mem_pool[j][:].indirect(member_list[:]), ACT.Copy)
+        def gather_values(j, on_scalar, reuse):
+            picked = tile([P, I], BF16, f"v_picked{j}", reuse)
+            if on_scalar:
+                nc.scalar.activation(picked[:], val_pool[j][:].indirect(slot_list[:]), ACT.Copy)
+            else:
+                nc.vector.tensor_copy(picked[:], val_pool[j][:].indirect(slot_list[:]))
+            return picked
+
+        def quantize_values(first, picked, bank, copy, reuse):
+            count = len(picked)
+            turned = ps.tile([P, count, 2, P], F32, name=f"v_turned{first}", tag=bank)
+            for n in range(count):
+                turn_pairs(picked[n][:], turned[:, n])
+            grouped = tile([P, count * P * PACK], BF16, f"v_grouped{first}", reuse)
+            copy(
+                grouped[:].bitcast(F32).rearrange("p (j c u) -> p j c u", j=count, u=2),
+                turned[:].rearrange("p j u c -> p j c u"),
+            )
+            cols = slice(first * P, (first + count) * P)
+            nc.vector.quantize_mx(v_codes[:, cols].bitcast(FP8X4), v_scales[:, cols], grouped[:])
+
+        quantize_values(0, [gather_values(0, True, None)], "values0", nc.vector.tensor_copy, None)
+        middle = [gather_values(1, True, "neg_best0"), gather_values(2, False, None)]
+        quantize_values(1, middle, "values1", nc.scalar.copy, "ratio1")
+        quantize_values(3, [gather_values(3, False, "p_inv1")], "values0", nc.scalar.copy, "root0")
+
+        gain_row = tile([P, Q], F32, "gain_row", "neg_best1")
+        gain_col = tile([P, HALVES], F32, "gain_col", "ratio0")
+        gain = tile([P, Q], F32, "gain")
+        nc.vector.tensor_copy(gain_row[:], gain_pool[:].indirect(member_list[:]))
+        gain_turned = ps.tile([P, HALVES, P], F32, name="gain_turned", tag="rows")
+        for h in range(HALVES):
+            nc.tensor.transpose(gain_turned[:, h, :], gain_row[:, h * P : (h + 1) * P], ident[:])
+        nc.scalar.copy(gain_col[:], gain_turned[:, :, 0])
+        gain_spread = ps.tile([P, Q], F32, name="gain_spread", tag="rows")
+        for h in range(HALVES):
+            nc.tensor.transpose(
+                gain_spread[:, h * P : (h + 1) * P], gain_col[:, h : h + 1].to_broadcast([P, P]), ident[:]
+            )
+        nc.scalar.copy(gain[:], gain_spread[:])
+
+        mem_picked = tile([P, PACK, Q], F32, "mem_picked", "root1")
+        for j in range(PACK):
+            nc.scalar.activation(mem_picked[:, j, :], mem_pool[j][:].indirect(member_list[:]), ACT.Copy)
         scaled = [tile([P, PACK, P], F32, f"scaled{h}") for h in range(HALVES)]
-        y = tile([P, PACK, Q], F32, "y")
+        y = [tile([P, PACK, P], F32, f"y{h}") for h in range(HALVES)]
         y_bf = [tile([P, P, PACK], BF16, f"y_bf{h}") for h in range(HALVES)]
         y_codes = tile([P, Q], U32, "y_codes")
         y_scales = tile([P, Q], U8, "y_scales")
@@ -282,13 +263,12 @@ def tile_attend_groupbest_overlinked_bymember_pl_kernel(
             cols = slice(h * P, (h + 1) * P)
             o = ps.tile([P, PACK, P], F32, name=f"o{h}", tag=f"product{h}")
             for j in range(PACK):
-                e_cols = slice((j % 2) * P, (j % 2 + 1) * P)
                 nc.tensor.matmul_mx(
                     o[:, j, :],
-                    lhsT=v_codes[j // 2][:, e_cols].bitcast(FP8X4),
-                    lhsT_scale=v_scales[j // 2][:, e_cols],
-                    rhs=w_codes[h][:].bitcast(FP8X4),
-                    rhs_scale=w_scales[h][:],
+                    lhsT=v_codes[:, j * P : (j + 1) * P].bitcast(FP8X4),
+                    lhsT_scale=v_scales[:, j * P : (j + 1) * P],
+                    rhs=w_codes[:, cols].bitcast(FP8X4),
+                    rhs_scale=w_scales[:, cols],
                     start=True,
                     stop=True,
                 )
@@ -298,22 +278,14 @@ def tile_attend_groupbest_overlinked_bymember_pl_kernel(
                 gain[:, cols].rearrange("p (o c) -> p o c", o=1).to_broadcast([P, PACK, P]),
                 ALU.mult,
             )
-            for (lo, hi, hold), picked in zip(runs, mem_picked):
-                nc.vector.tensor_tensor(y[:, lo:hi, cols], picked[:, :, cols], scaled[h][:, lo:hi, :], ALU.add)
-            for j in range(dense, PACK):
-                if True:
-                    addend = mem_pool[j][:].indirect(member_list[:, 8 * h : 8 * (h + 1)])
-                    nc.vector.tensor_tensor(y[:, j, cols], addend, scaled[h][:, j, :], ALU.add)
-            nc.sync.dma_start(out_dealt[:, :, cols], y[:, :, cols])
-            src = y[:, :, cols].rearrange("p t (c i) -> p c t i", i=4)
-            dst = y_bf[h][:].rearrange("p (c i) t -> p c t i", i=4)
-            [nc.scalar.copy, nc.vector.tensor_copy][h](dst, src)
-        nc.vector.quantize_mx(
-            y_codes[:, :P].bitcast(FP8X4), y_scales[:, :P], y_bf[0][:].rearrange("p c t -> p (c t)")
-        )
-        nc.vector.quantize_mx(
-            y_codes[:, P:].bitcast(FP8X4), y_scales[:, P:], y_bf[1][:].rearrange("p c t -> p (c t)")
-        )
+            nc.vector.tensor_tensor(y[h][:], mem_picked[:, :, cols], scaled[h][:], ALU.add)
+            nc.sync.dma_start(out_dealt[:, :, cols], y[h][:])
+            [nc.scalar.copy, nc.vector.tensor_copy][h](
+                y_bf[h][:].rearrange("p (c i) t -> p c t i", i=4), y[h][:].rearrange("p t (c i) -> p c t i", i=4)
+            )
+            nc.vector.quantize_mx(
+                y_codes[:, cols].bitcast(FP8X4), y_scales[:, cols], y_bf[h][:].rearrange("p c t -> p (c t)")
+            )
         nc.sync.dma_start(out_1[0].rearrange("p c r -> p (c r)").bitcast(I32), y_codes[:].bitcast(I32))
         for quad in range(4):
             nc.scalar.dma_start(

@@ -44,9 +44,8 @@ def tile_attend_groupbest_overlinked_bymember_pl_kernel(
         key_words = tile([P, T], U16, "key_words")
         key_scales = tile([P, T], U8, "key_scales")
         q_raw = tile([P, PACK, Q], F32, "q_raw")
-        lam_col = tile([P, HALVES], F32, "lam_col")
-        rival_col = tile([P, HALVES], F32, "rival_col")
-        factor_col = tile([P, PACK], F32, "factor_col")
+        lam_row = tile([P, Q], F32, "lam_row")
+        late_rows = tile([P, I], F32, "late_rows")
         gain_pool = tile([P, M], F32, "gain_pool")
         val_pool = [tile([P, T], F32, f"val_pool{j}") for j in range(PACK)]
         mem_pool = [tile([P, M], F32, f"mem_pool{j}") for j in range(PACK)]
@@ -55,6 +54,8 @@ def tile_attend_groupbest_overlinked_bymember_pl_kernel(
         member_dealt = member.rearrange("(p j) m -> j p m", j=PACK)
 
         nc.vector.memset(key_scales[:].bitcast(I32), 0)
+        nc.vector.memset(lam_row[:], 0.0)
+        nc.vector.memset(late_rows[:], 0.0)
         nc.vector.memset(gain_pool[:], 0.0)
         make_identity(nc, ident[:])
         nc.sync.dma_start(slot_list[:], offs)
@@ -65,17 +66,15 @@ def tile_attend_groupbest_overlinked_bymember_pl_kernel(
                 key_scales[32 * quad : 32 * quad + 4, :].bitcast(I32),
                 keys_scales[0, 4 * quad : 4 * quad + 4, :].bitcast(I32),
             )
-        with nc.allow_non_contiguous_dma(reason="one value to a partition"):
-            nc.sync.dma_start(lam_col[:], lam.rearrange("o (h p) -> p (o h)", p=P))
+        nc.sync.dma_start(lam_row[0:1, :], lam)
         nc.sync.dma_start(val_pool[0][:], vals_dealt[0])
         nc.sync.dma_start(member_list[:], offs2)
         nc.sync.dma_start(gain_pool[0:1, :], mgain[0:1, :])
         nc.sync.dma_start(val_pool[1][:], vals_dealt[1])
         nc.sync.dma_start(rival_list[:], offs4)
         nc.sync.dma_start(val_pool[2][:], vals_dealt[2])
-        with nc.allow_non_contiguous_dma(reason="one value to a partition"):
-            nc.sync.dma_start(rival_col[:], rival.rearrange("(h p) o -> p (h o)", p=P))
-        nc.sync.dma_start(factor_col[:], slot_factor.rearrange("o (p t) -> p (o t)", t=PACK))
+        nc.sync.dma_start(late_rows[0:1, :], slot_factor)
+        nc.sync.dma_start(late_rows[1:2, 0:Q], rival.rearrange("q o -> o q"))
         nc.sync.dma_start(val_pool[3][:], vals_dealt[3])
         for j in range(PACK):
             nc.sync.dma_start(mem_pool[j][:], member_dealt[j])
@@ -94,10 +93,19 @@ def tile_attend_groupbest_overlinked_bymember_pl_kernel(
         for b in range(2):
             nc.vector.tensor_copy(k_words[b][:], key_words[:].indirect(slot_list[:, 16 * b : 16 * (b + 1)]))
 
+        def rows_to_columns(rows, blocks, live, name, bank, copy, reuse=None):
+            turned = ps.tile([P, blocks, P], F32, name=f"{name}_turned", tag=bank)
+            for c in range(blocks):
+                nc.tensor.transpose(turned[:, c, :], rows[:, c * P : (c + 1) * P], ident[:])
+            columns = tile([P, blocks, live], F32, name, reuse)
+            copy(columns[:], turned[:, :, 0:live])
+            return columns
+
+        lam_col = rows_to_columns(lam_row, HALVES, 1, "lam_col", "factor_rows", nc.scalar.copy)
         lam_turned = ps.tile([P, Q], F32, name="lam_turned", tag="rows")
         for h in range(HALVES):
             nc.tensor.transpose(
-                lam_turned[:, h * P : (h + 1) * P], lam_col[:, h : h + 1].to_broadcast([P, P]), ident[:]
+                lam_turned[:, h * P : (h + 1) * P], lam_col[:, h, :].to_broadcast([P, P]), ident[:]
             )
 
         raw = [ps.tile([P, 2, Q], F32, name=f"raw{b}", tag=f"product{b}") for b in range(2)]
@@ -164,9 +172,12 @@ def tile_attend_groupbest_overlinked_bymember_pl_kernel(
                     ALU.mult,
                 )
 
-        factor_rows = ps.tile([P, PACK, P], F32, name="factor_rows", tag="factor_rows")
-        for t in range(PACK):
-            nc.tensor.transpose(factor_rows[:, t, :], factor_col[:, t : t + 1].to_broadcast([P, P]), ident[:])
+        late_cols = rows_to_columns(late_rows, I // P, 2, "late_cols", "factor_rows", nc.vector.tensor_copy)
+        factor_rows = ps.tile([P, I], F32, name="factor_rows", tag="factor_rows")
+        for c in range(I // P):
+            nc.tensor.transpose(
+                factor_rows[:, c * P : (c + 1) * P], late_cols[:, c, 0:1].to_broadcast([P, P]), ident[:]
+            )
 
         root = [tile([P, I], F32, f"root{h}") for h in range(HALVES)]
         part = [tile([P, I], F32, f"part{h}") for h in range(HALVES)]
@@ -177,7 +188,7 @@ def tile_attend_groupbest_overlinked_bymember_pl_kernel(
         w_scales = tile([P, Q], U8, "w_scales")
         for h in range(HALVES):
             nc.scalar.activation(
-                root[h][:], ratio[h][:], ACT.Abs_reciprocal_sqrt, scale=rival_col[:, h : h + 1], bias=1.0
+                root[h][:], ratio[h][:], ACT.Abs_reciprocal_sqrt, scale=late_cols[:, h, 1:2], bias=1.0
             )
         for h in range(HALVES):
             nc.scalar.activation(part[h][:], root[h][:], ACT.Square, accum_out=part_sum[h][:])
@@ -191,10 +202,10 @@ def tile_attend_groupbest_overlinked_bymember_pl_kernel(
             cols = slice(h * P, (h + 1) * P)
             nc.vector.reciprocal(inv_sum[h][:], part_sum[h][:])
             nc.vector.scalar_tensor_tensor(
-                w_bf[h][:].rearrange("q (p t) -> q p t", t=PACK),
-                part[h][:].rearrange("q (p t) -> q p t", t=PACK),
+                w_bf[h][:],
+                part[h][:],
                 inv_sum[h][:],
-                factor_rows[:].rearrange("q t p -> q p t"),
+                factor_rows[:],
                 ALU.mult,
                 ALU.mult,
             )

@@ -44,8 +44,9 @@ def tile_attend_groupbest_overlinked_bymember_pl_kernel(
         key_words = tile([P, T], U16, "key_words")
         key_scales = tile([P, T], U8, "key_scales")
         q_raw = tile([P, PACK, Q], F32, "q_raw")
-        lam_row = tile([P, Q], F32, "lam_row")
-        late_rows = tile([P, I], F32, "late_rows")
+        lam_col = tile([P, HALVES], F32, "lam_col")
+        rival_col = tile([P, HALVES], F32, "rival_col")
+        factor_col = tile([P, PACK], F32, "factor_col")
         gain_pool = tile([P, M], F32, "gain_pool")
         val_pool = [tile([P, T], F32, f"val_pool{j}") for j in range(PACK)]
         mem_pool = [tile([P, M], F32, f"mem_pool{j}") for j in range(PACK)]
@@ -54,8 +55,6 @@ def tile_attend_groupbest_overlinked_bymember_pl_kernel(
         member_dealt = member.rearrange("(p j) m -> j p m", j=PACK)
 
         nc.vector.memset(key_scales[:].bitcast(I32), 0)
-        nc.vector.memset(lam_row[:], 0.0)
-        nc.vector.memset(late_rows[:], 0.0)
         nc.vector.memset(gain_pool[:], 0.0)
         make_identity(nc, ident[:])
         nc.sync.dma_start(slot_list[:], offs)
@@ -66,15 +65,17 @@ def tile_attend_groupbest_overlinked_bymember_pl_kernel(
                 key_scales[32 * quad : 32 * quad + 4, :].bitcast(I32),
                 keys_scales[0, 4 * quad : 4 * quad + 4, :].bitcast(I32),
             )
-        nc.sync.dma_start(lam_row[0:1, :], lam)
+        with nc.allow_non_contiguous_dma(reason="one value to a partition"):
+            nc.sync.dma_start(lam_col[:], lam.rearrange("o (h p) -> p (o h)", p=P))
         nc.sync.dma_start(val_pool[0][:], vals_dealt[0])
         nc.sync.dma_start(member_list[:], offs2)
         nc.sync.dma_start(gain_pool[0:1, :], mgain[0:1, :])
         nc.sync.dma_start(val_pool[1][:], vals_dealt[1])
         nc.sync.dma_start(rival_list[:], offs4)
         nc.sync.dma_start(val_pool[2][:], vals_dealt[2])
-        nc.sync.dma_start(late_rows[0:1, :], slot_factor)
-        nc.sync.dma_start(late_rows[1:2, 0:Q], rival.rearrange("q o -> o q"))
+        with nc.allow_non_contiguous_dma(reason="one value to a partition"):
+            nc.sync.dma_start(rival_col[:], rival.rearrange("(h p) o -> p (h o)", p=P))
+        nc.sync.dma_start(factor_col[:], slot_factor.rearrange("o (p t) -> p (o t)", t=PACK))
         nc.sync.dma_start(val_pool[3][:], vals_dealt[3])
         for j in range(PACK):
             nc.sync.dma_start(mem_pool[j][:], member_dealt[j])
@@ -93,19 +94,10 @@ def tile_attend_groupbest_overlinked_bymember_pl_kernel(
         for b in range(2):
             nc.vector.tensor_copy(k_words[b][:], key_words[:].indirect(slot_list[:, 16 * b : 16 * (b + 1)]))
 
-        def rows_to_columns(rows, blocks, live, name, bank, copy, reuse=None):
-            turned = ps.tile([P, blocks, P], F32, name=f"{name}_turned", tag=bank)
-            for c in range(blocks):
-                nc.tensor.transpose(turned[:, c, :], rows[:, c * P : (c + 1) * P], ident[:])
-            columns = tile([P, blocks, live], F32, name, reuse)
-            copy(columns[:], turned[:, :, 0:live])
-            return columns
-
-        lam_col = rows_to_columns(lam_row, HALVES, 1, "lam_col", "factor_rows", nc.scalar.copy)
         lam_turned = ps.tile([P, Q], F32, name="lam_turned", tag="rows")
         for h in range(HALVES):
             nc.tensor.transpose(
-                lam_turned[:, h * P : (h + 1) * P], lam_col[:, h, :].to_broadcast([P, P]), ident[:]
+                lam_turned[:, h * P : (h + 1) * P], lam_col[:, h : h + 1].to_broadcast([P, P]), ident[:]
             )
 
         raw = [ps.tile([P, 2, Q], F32, name=f"raw{b}", tag=f"product{b}") for b in range(2)]
@@ -172,23 +164,20 @@ def tile_attend_groupbest_overlinked_bymember_pl_kernel(
                     ALU.mult,
                 )
 
-        late_cols = rows_to_columns(late_rows, I // P, 2, "late_cols", "factor_rows", nc.vector.tensor_copy)
-        factor_rows = ps.tile([P, I], F32, name="factor_rows", tag="factor_rows")
-        for c in range(I // P):
-            nc.tensor.transpose(
-                factor_rows[:, c * P : (c + 1) * P], late_cols[:, c, 0:1].to_broadcast([P, P]), ident[:]
-            )
+        factor_rows = ps.tile([P, PACK, P], F32, name="factor_rows", tag="factor_rows")
+        for t in range(PACK):
+            nc.tensor.transpose(factor_rows[:, t, :], factor_col[:, t : t + 1].to_broadcast([P, P]), ident[:])
 
         root = [tile([P, I], F32, f"root{h}") for h in range(HALVES)]
         part = [tile([P, I], F32, f"part{h}") for h in range(HALVES)]
         part_sum = [tile([P, 1], F32, f"part_sum{h}") for h in range(HALVES)]
         inv_sum = [tile([P, 1], F32, f"inv_sum{h}") for h in range(HALVES)]
-        w_bf = [tile([P, I], BF16, f"w_bf{h}") for h in range(HALVES)]
+        w_bf = [tile([P, 2, P, 2], BF16, f"w_bf{h}") for h in range(HALVES)]
         w_codes = tile([P, Q], U32, "w_codes")
         w_scales = tile([P, Q], U8, "w_scales")
         for h in range(HALVES):
             nc.scalar.activation(
-                root[h][:], ratio[h][:], ACT.Abs_reciprocal_sqrt, scale=late_cols[:, h, 1:2], bias=1.0
+                root[h][:], ratio[h][:], ACT.Abs_reciprocal_sqrt, scale=rival_col[:, h : h + 1], bias=1.0
             )
         for h in range(HALVES):
             nc.scalar.activation(part[h][:], root[h][:], ACT.Square, accum_out=part_sum[h][:])
@@ -201,16 +190,19 @@ def tile_attend_groupbest_overlinked_bymember_pl_kernel(
         for h in range(HALVES):
             cols = slice(h * P, (h + 1) * P)
             nc.vector.reciprocal(inv_sum[h][:], part_sum[h][:])
-            nc.vector.scalar_tensor_tensor(
-                w_bf[h][:],
-                part[h][:],
-                inv_sum[h][:],
-                factor_rows[:],
-                ALU.mult,
-                ALU.mult,
-            )
             w_turned = ps.tile([P, 2, P], F32, name=f"w_turned{h}", tag=f"turn{h}")
-            turn_pairs(w_bf[h][:], w_turned)
+            for u in range(2):
+                nc.vector.scalar_tensor_tensor(
+                    w_bf[h][:, u],
+                    part[h][:].rearrange("q (p u e) -> q u p e", u=2, e=2)[:, u],
+                    inv_sum[h][:],
+                    factor_rows[:, 2 * u : 2 * u + 2, :].rearrange("q e p -> q p e"),
+                    ALU.mult,
+                    ALU.mult,
+                )
+                nc.tensor.transpose(
+                    w_turned[:, u, :], w_bf[h][:, u].rearrange("q p e -> q (p e)").bitcast(F32), ident[:]
+                )
             w_grouped = tile([P, P * PACK], BF16, f"w_grouped{h}")
             nc.vector.tensor_copy(
                 w_grouped[:].bitcast(F32).rearrange("p (c u) -> p c u", u=2), w_turned[:].rearrange("p u c -> p c u")
@@ -247,13 +239,13 @@ def tile_attend_groupbest_overlinked_bymember_pl_kernel(
         quantize_values(3, [gather_values(3, False, "p_inv1")], "values0", nc.scalar.copy, "root0")
 
         gain_row = tile([P, Q], F32, "gain_row", "neg_best1")
-        gain_col = tile([P, HALVES], F32, "gain_col", "ratio0")
-        gain = tile([P, Q], F32, "gain")
+        gain_col = tile([P, HALVES], F32, "gain_col")
+        gain = tile([P, Q], F32, "gain", "ratio0")
         nc.vector.tensor_copy(gain_row[:], gain_pool[:].indirect(member_list[:]))
         gain_turned = ps.tile([P, HALVES, P], F32, name="gain_turned", tag="rows")
         for h in range(HALVES):
             nc.tensor.transpose(gain_turned[:, h, :], gain_row[:, h * P : (h + 1) * P], ident[:])
-        nc.scalar.copy(gain_col[:], gain_turned[:, :, 0])
+        nc.vector.tensor_copy(gain_col[:], gain_turned[:, :, 0])
         gain_spread = ps.tile([P, Q], F32, name="gain_spread", tag="rows")
         for h in range(HALVES):
             nc.tensor.transpose(
@@ -291,15 +283,18 @@ def tile_attend_groupbest_overlinked_bymember_pl_kernel(
             )
             nc.vector.tensor_tensor(y[h][:], mem_picked[:, :, cols], scaled[h][:], ALU.add)
             nc.sync.dma_start(out_dealt[:, :, cols], y[h][:])
-            [nc.scalar.copy, nc.vector.tensor_copy][h](
-                y_bf[h][:].rearrange("p (c i) t -> p c t i", i=4), y[h][:].rearrange("p t (c i) -> p c t i", i=4)
-            )
+            y_src = y[h][:].rearrange("p t (c i) -> p c t i", i=4)
+            y_dst = y_bf[h][:].rearrange("p (c i) t -> p c t i", i=4)
+            scalar_share = [32, 10][h]
+            nc.scalar.copy(y_dst[:, :scalar_share], y_src[:, :scalar_share])
+            if scalar_share < 32:
+                nc.vector.tensor_copy(y_dst[:, scalar_share:], y_src[:, scalar_share:])
             nc.vector.quantize_mx(
                 y_codes[:, cols].bitcast(FP8X4), y_scales[:, cols], y_bf[h][:].rearrange("p c t -> p (c t)")
             )
-        nc.sync.dma_start(out_1[0].rearrange("p c r -> p (c r)").bitcast(I32), y_codes[:].bitcast(I32))
+        nc.scalar.dma_start(out_1[0].rearrange("p c r -> p (c r)").bitcast(I32), y_codes[:].bitcast(I32))
         for quad in range(4):
-            nc.scalar.dma_start(
+            [nc.sync, nc.scalar][quad % 2].dma_start(
                 out_2[0, 4 * quad : 4 * quad + 4, :].bitcast(I32),
                 y_scales[32 * quad : 32 * quad + 4, :].bitcast(I32),
             )

@@ -24,6 +24,11 @@ PACK = 4
 HALVES = Q // P
 GROUPS = Q // GROUP
 LIST_ROWS = 16
+QUADRANTS = 4
+RUN = 4
+BANK_BLOCKS = 2
+SLOT_BANKS = I // (BANK_BLOCKS * P)
+LAST_SCALAR_RUNS = 10
 
 
 def tile_attend_groupbest_overlinked_bymember_pl_kernel(
@@ -60,7 +65,7 @@ def tile_attend_groupbest_overlinked_bymember_pl_kernel(
         nc.sync.dma_start(slot_list[:], offs)
         nc.sync.dma_start(key_words[:].bitcast(I32), keys_words[0].bitcast(I32))
         nc.sync.dma_start(q_raw[:], query.rearrange("(p j) q -> p j q", j=PACK))
-        for quad in range(4):
+        for quad in range(QUADRANTS):
             nc.sync.dma_start(
                 key_scales[32 * quad : 32 * quad + 4, :].bitcast(I32),
                 keys_scales[0, 4 * quad : 4 * quad + 4, :].bitcast(I32),
@@ -80,19 +85,23 @@ def tile_attend_groupbest_overlinked_bymember_pl_kernel(
         for j in range(PACK):
             nc.sync.dma_start(mem_pool[j][:], member_dealt[j])
 
-        k_words = [tile([P, 2 * P], U16, f"k_words{b}") for b in range(2)]
+        k_words = [tile([P, BANK_BLOCKS * P], U16, f"k_words{b}") for b in range(SLOT_BANKS)]
         k_scales = tile([P, I], U8, "k_scales")
         q_bf = tile([P, Q, PACK], BF16, "q_bf")
         q_codes = tile([P, Q], U32, "q_codes")
         q_scales = tile([P, Q], U8, "q_scales")
 
         nc.scalar.activation(
-            q_bf[:].rearrange("p (c i) t -> p c t i", i=4), q_raw[:].rearrange("p t (c i) -> p c t i", i=4), ACT.Copy
+            q_bf[:].rearrange("p (c i) t -> p c t i", i=RUN),
+            q_raw[:].rearrange("p t (c i) -> p c t i", i=RUN),
+            ACT.Copy,
         )
         nc.vector.quantize_mx(q_codes[:].bitcast(FP8X4), q_scales[:], q_bf[:].rearrange("p c t -> p (c t)"))
         nc.vector.tensor_copy(k_scales[:], key_scales[:].indirect(slot_list[:]))
-        for b in range(2):
-            nc.vector.tensor_copy(k_words[b][:], key_words[:].indirect(slot_list[:, 16 * b : 16 * (b + 1)]))
+        bank_cols = BANK_BLOCKS * P // LIST_ROWS
+        for b in range(SLOT_BANKS):
+            bank_list = slot_list[:, bank_cols * b : bank_cols * (b + 1)]
+            nc.vector.tensor_copy(k_words[b][:], key_words[:].indirect(bank_list))
 
         lam_turned = ps.tile([P, Q], F32, name="lam_turned", tag="rows")
         for h in range(HALVES):
@@ -100,10 +109,10 @@ def tile_attend_groupbest_overlinked_bymember_pl_kernel(
                 lam_turned[:, h * P : (h + 1) * P], lam_col[:, h : h + 1].to_broadcast([P, P]), ident[:]
             )
 
-        raw = [ps.tile([P, 2, Q], F32, name=f"raw{b}", tag=f"product{b}") for b in range(2)]
-        for b in range(2):
-            for c in range(2):
-                block = 2 * b + c
+        raw = [ps.tile([P, BANK_BLOCKS, Q], F32, name=f"raw{b}", tag=f"product{b}") for b in range(SLOT_BANKS)]
+        for b in range(SLOT_BANKS):
+            for c in range(BANK_BLOCKS):
+                block = BANK_BLOCKS * b + c
                 nc.tensor.matmul_mx(
                     raw[b][:, c, :],
                     lhsT=k_words[b][:, c * P : (c + 1) * P].bitcast(FP4X4),
@@ -114,11 +123,12 @@ def tile_attend_groupbest_overlinked_bymember_pl_kernel(
                     stop=True,
                 )
 
-        lam_rows = lam_turned[:].rearrange("p (o v g) -> p o v g", o=1, g=GROUP).to_broadcast([P, 2, GROUPS, GROUP])
-        raw_sb = [tile([P, 2, Q], F32, f"raw_sb{b}") for b in range(2)]
-        shift = [tile([P, 2, GROUPS, GROUP], F32, f"shift{b}") for b in range(2)]
-        neg_best = [tile([P, 2, GROUPS, 1], F32, f"neg_best{b}") for b in range(2)]
-        for b in range(2):
+        by_group = [P, BANK_BLOCKS, GROUPS, GROUP]
+        lam_rows = lam_turned[:].rearrange("p (o v g) -> p o v g", o=1, g=GROUP).to_broadcast(by_group)
+        raw_sb = [tile([P, BANK_BLOCKS, Q], F32, f"raw_sb{b}") for b in range(SLOT_BANKS)]
+        shift = [tile(by_group, F32, f"shift{b}") for b in range(SLOT_BANKS)]
+        neg_best = [tile([P, BANK_BLOCKS, GROUPS, 1], F32, f"neg_best{b}") for b in range(SLOT_BANKS)]
+        for b in range(SLOT_BANKS):
             nc.vector.tensor_reduce(
                 neg_best[b][:].rearrange("p c v o -> p (c v o)"),
                 raw[b][:].rearrange("p c (v g) -> p (c v) g", g=GROUP),
@@ -127,25 +137,23 @@ def tile_attend_groupbest_overlinked_bymember_pl_kernel(
                 negate=True,
             )
             nc.scalar.copy(raw_sb[b][:], raw[b][:])
-        for b in range(2):
-            nc.vector.tensor_tensor(
-                shift[b][:], neg_best[b][:].to_broadcast([P, 2, GROUPS, GROUP]), lam_rows, ALU.mult
-            )
+        for b in range(SLOT_BANKS):
+            nc.vector.tensor_tensor(shift[b][:], neg_best[b][:].to_broadcast(by_group), lam_rows, ALU.mult)
 
         score = [ps.tile([P, I], F32, name=f"score{h}", tag=f"turn{h}") for h in range(HALVES)]
         for h in range(HALVES):
-            for b in range(2):
+            for b in range(SLOT_BANKS):
                 terms = [raw_sb[b][:], shift[b][:].rearrange("p c v g -> p c (v g)")]
                 for n, term in enumerate(terms):
-                    for c in range(2):
-                        block = 2 * b + c
+                    for c in range(BANK_BLOCKS):
+                        block = BANK_BLOCKS * b + c
                         nc.tensor.matmul(
                             score[h][:, block * P : (block + 1) * P],
                             lhsT=term[:, c, h * P : (h + 1) * P],
                             rhs=ident[:],
                             is_transpose=True,
                             start=(b == 0 and n == 0 and c == 0),
-                            stop=(b == 1 and n == 1 and c == 1),
+                            stop=(b == SLOT_BANKS - 1 and n == len(terms) - 1 and c == BANK_BLOCKS - 1),
                         )
 
         p_sb = [tile([P, I], F32, f"p{h}") for h in range(HALVES)]
@@ -154,12 +162,13 @@ def tile_attend_groupbest_overlinked_bymember_pl_kernel(
         for h in range(HALVES):
             nc.scalar.activation(p_sb[h][:], score[h][:], ACT.Exp)
             nc.scalar.activation(p_inv[h][:], score[h][:], ACT.Exp, scale=-1.0)
+        piece = I // 2
         for h in range(HALVES):
-            for c in range(2):
-                cols = slice(c * I // 2, (c + 1) * I // 2)
+            for first in range(0, I, piece):
+                cols = slice(first, first + piece)
                 nc.vector.tensor_tensor(
                     ratio[h][:, cols],
-                    p_sb[h][:].indirect(rival_list[:, 16 * c : 16 * (c + 1)]),
+                    p_sb[h][:].indirect(rival_list[:, first // LIST_ROWS : (first + piece) // LIST_ROWS]),
                     p_inv[h][:, cols],
                     ALU.mult,
                 )
@@ -181,11 +190,6 @@ def tile_attend_groupbest_overlinked_bymember_pl_kernel(
             )
         for h in range(HALVES):
             nc.scalar.activation(part[h][:], root[h][:], ACT.Square, accum_out=part_sum[h][:])
-
-        def turn_pairs(rows_bf, turned):
-            pairs = rows_bf.bitcast(F32)
-            for u in range(2):
-                nc.tensor.transpose(turned[:, u, :], pairs[:, u : I // 2 : 2], ident[:])
 
         for h in range(HALVES):
             cols = slice(h * P, (h + 1) * P)
@@ -211,6 +215,11 @@ def tile_attend_groupbest_overlinked_bymember_pl_kernel(
 
         v_codes = tile([P, E], U32, "v_codes")
         v_scales = tile([P, E], U8, "v_scales")
+
+        def turn_pairs(rows_bf, turned):
+            pairs = rows_bf.bitcast(F32)
+            for u in range(2):
+                nc.tensor.transpose(turned[:, u, :], pairs[:, u : I // 2 : 2], ident[:])
 
         def gather_values(j, on_scalar, reuse):
             picked = tile([P, I], BF16, f"v_picked{j}", reuse)
@@ -253,9 +262,12 @@ def tile_attend_groupbest_overlinked_bymember_pl_kernel(
             )
         nc.scalar.copy(gain[:], gain_spread[:])
 
-        mem_picked = tile([P, PACK, Q], F32, "mem_picked", "root1")
-        for j in range(PACK):
-            nc.scalar.activation(mem_picked[:, j, :], mem_pool[j][:].indirect(member_list[:]), ACT.Copy)
+        mem_picked = tile([P, HALVES, PACK, P], F32, "mem_picked", "root1")
+        half_cols = P // LIST_ROWS
+        for h in range(HALVES):
+            for j in range(PACK):
+                listed = mem_pool[j][:].indirect(member_list[:, half_cols * h : half_cols * (h + 1)])
+                nc.scalar.activation(mem_picked[:, h, j, :], listed, ACT.Copy)
         scaled = [tile([P, PACK, P], F32, f"scaled{h}") for h in range(HALVES)]
         y = [tile([P, PACK, P], F32, f"y{h}") for h in range(HALVES)]
         y_bf = [tile([P, P, PACK], BF16, f"y_bf{h}") for h in range(HALVES)]
@@ -281,19 +293,20 @@ def tile_attend_groupbest_overlinked_bymember_pl_kernel(
                 gain[:, cols].rearrange("p (o c) -> p o c", o=1).to_broadcast([P, PACK, P]),
                 ALU.mult,
             )
-            nc.vector.tensor_tensor(y[h][:], mem_picked[:, :, cols], scaled[h][:], ALU.add)
+            nc.vector.tensor_tensor(y[h][:], mem_picked[:, h], scaled[h][:], ALU.add)
             nc.sync.dma_start(out_dealt[:, :, cols], y[h][:])
-            y_src = y[h][:].rearrange("p t (c i) -> p c t i", i=4)
-            y_dst = y_bf[h][:].rearrange("p (c i) t -> p c t i", i=4)
-            scalar_share = [32, 10][h]
-            nc.scalar.copy(y_dst[:, :scalar_share], y_src[:, :scalar_share])
-            if scalar_share < 32:
-                nc.vector.tensor_copy(y_dst[:, scalar_share:], y_src[:, scalar_share:])
+            y_src = y[h][:].rearrange("p t (c i) -> p c t i", i=RUN)
+            y_dst = y_bf[h][:].rearrange("p (c i) t -> p c t i", i=RUN)
+            if h < HALVES - 1:
+                nc.scalar.copy(y_dst, y_src)
+            else:
+                nc.scalar.copy(y_dst[:, :LAST_SCALAR_RUNS], y_src[:, :LAST_SCALAR_RUNS])
+                nc.vector.tensor_copy(y_dst[:, LAST_SCALAR_RUNS:], y_src[:, LAST_SCALAR_RUNS:])
             nc.vector.quantize_mx(
                 y_codes[:, cols].bitcast(FP8X4), y_scales[:, cols], y_bf[h][:].rearrange("p c t -> p (c t)")
             )
         nc.scalar.dma_start(out_1[0].rearrange("p c r -> p (c r)").bitcast(I32), y_codes[:].bitcast(I32))
-        for quad in range(4):
+        for quad in range(QUADRANTS):
             [nc.sync, nc.scalar][quad % 2].dma_start(
                 out_2[0, 4 * quad : 4 * quad + 4, :].bitcast(I32),
                 y_scales[32 * quad : 32 * quad + 4, :].bitcast(I32),

from contextlib import ExitStack

import concourse.mybir as mybir
from concourse.masks import make_identity

D, T, I, Q, E, M = 512, 2048, 512, 256, 512, 1024
GROUP = 8
FLOPS = 2 * D * I * Q + 2 * I * E * Q

F32 = mybir.dt.float32
BF16 = mybir.dt.bfloat16
I32 = mybir.dt.int32
U32 = mybir.dt.uint32
U16 = mybir.dt.uint16
U8 = mybir.dt.uint8
FP8X4 = mybir.dt.float8_e4m3fn_x4
FP4X4 = mybir.dt.float4_e2m1fn_x4
ACT = mybir.ActivationFunctionType
ALU = mybir.AluOpType
AXIS = mybir.AxisListType

P = 128
PACK = 4
HALVES = Q // P
GROUPS = Q // GROUP
LIST_ROWS = 16
QUADRANTS = 4
RUN = 4
BANK_BLOCKS = 2
SLOT_BANKS = I // (BANK_BLOCKS * P)
LAST_SCALAR_RUNS = 10


def tile_attend_groupbest_overlinked_bymember_pl_kernel(
    tc, query, keys_words, keys_scales, lam, rival, slot_factor, vals, member, mgain, offs, offs2, offs4,
    out_0, out_1, out_2,
):
    nc = tc.nc
    with ExitStack() as ctx:
        sb = ctx.enter_context(tc.tile_pool(name="sb", bufs=1))
        ps = ctx.enter_context(tc.psum_pool(name="ps", bufs=1))

        def tile(shape, dtype, name, reuse=None):
            return sb.tile(shape, dtype, name=name, tag=reuse or name, align_bytes=64)

        slot_list = sb.tile([P, I // LIST_ROWS], U16, name="slot_list")
        member_list = sb.tile([P, Q // LIST_ROWS], U16, name="member_list")
        rival_list = sb.tile([P, I // LIST_ROWS], U16, name="rival_list")
        key_words = tile([P, T], U16, "key_words")
        key_scales = tile([P, T], U8, "key_scales")
        q_raw = tile([P, PACK, Q], F32, "q_raw")
        lam_col = tile([P, HALVES], F32, "lam_col")
        rival_col = tile([P, HALVES], F32, "rival_col")
        factor_col = tile([P, PACK], F32, "factor_col")
        gain_pool = tile([P, M], F32, "gain_pool")
        val_pool = [tile([P, T], F32, f"val_pool{j}") for j in range(PACK)]
        mem_pool = [tile([P, M], F32, f"mem_pool{j}") for j in range(PACK)]
        ident = tile([P, P], F32, "ident")
        vals_dealt = vals.rearrange("(p j) t -> j p t", j=PACK)
        member_dealt = member.rearrange("(p j) m -> j p m", j=PACK)

        nc.vector.memset(key_scales[:].bitcast(I32), 0)
        nc.vector.memset(gain_pool[:], 0.0)
        make_identity(nc, ident[:])
        nc.sync.dma_start(slot_list[:], offs)
        nc.sync.dma_start(key_words[:].bitcast(I32), keys_words[0].bitcast(I32))
        nc.sync.dma_start(q_raw[:], query.rearrange("(p j) q -> p j q", j=PACK))
        for quad in range(QUADRANTS):
            nc.sync.dma_start(
                key_scales[32 * quad : 32 * quad + 4, :].bitcast(I32),
                keys_scales[0, 4 * quad : 4 * quad + 4, :].bitcast(I32),
            )
        with nc.allow_non_contiguous_dma(reason="one value to a partition"):
            nc.sync.dma_start(lam_col[:], lam.rearrange("o (h p) -> p (o h)", p=P))
        nc.sync.dma_start(val_pool[0][:], vals_dealt[0])
        nc.sync.dma_start(member_list[:], offs2)
        nc.sync.dma_start(gain_pool[0:1, :], mgain[0:1, :])
        nc.sync.dma_start(val_pool[1][:], vals_dealt[1])
        nc.sync.dma_start(rival_list[:], offs4)
        nc.sync.dma_start(val_pool[2][:], vals_dealt[2])
        with nc.allow_non_contiguous_dma(reason="one value to a partition"):
            nc.sync.dma_start(rival_col[:], rival.rearrange("(h p) o -> p (h o)", p=P))
        nc.sync.dma_start(factor_col[:], slot_factor.rearrange("o (p t) -> p (o t)", t=PACK))
        nc.sync.dma_start(val_pool[3][:], vals_dealt[3])
        for j in range(PACK):
            nc.sync.dma_start(mem_pool[j][:], member_dealt[j])

        k_words = [tile([P, BANK_BLOCKS * P], U16, f"k_words{b}") for b in range(SLOT_BANKS)]
        k_scales = tile([P, I], U8, "k_scales")
        q_bf = tile([P, Q, PACK], BF16, "q_bf")
        q_codes = tile([P, Q], U32, "q_codes")
        q_scales = tile([P, Q], U8, "q_scales")

        nc.scalar.activation(
            q_bf[:].rearrange("p (c i) t -> p c t i", i=RUN),
            q_raw[:].rearrange("p t (c i) -> p c t i", i=RUN),
            ACT.Copy,
        )
        nc.vector.quantize_mx(q_codes[:].bitcast(FP8X4), q_scales[:], q_bf[:].rearrange("p c t -> p (c t)"))
        nc.vector.tensor_copy(k_scales[:], key_scales[:].indirect(slot_list[:]))
        bank_cols = BANK_BLOCKS * P // LIST_ROWS
        for b in range(SLOT_BANKS):
            bank_list = slot_list[:, bank_cols * b : bank_cols * (b + 1)]
            nc.vector.tensor_copy(k_words[b][:], key_words[:].indirect(bank_list))

        lam_turned = ps.tile([P, Q], F32, name="lam_turned", tag="rows")
        for h in range(HALVES):
            nc.tensor.transpose(
                lam_turned[:, h * P : (h + 1) * P], lam_col[:, h : h + 1].to_broadcast([P, P]), ident[:]
            )

        raw = [ps.tile([P, BANK_BLOCKS, Q], F32, name=f"raw{b}", tag=f"product{b}") for b in range(SLOT_BANKS)]
        for b in range(SLOT_BANKS):
            for c in range(BANK_BLOCKS):
                block = BANK_BLOCKS * b + c
                nc.tensor.matmul_mx(
                    raw[b][:, c, :],
                    lhsT=k_words[b][:, c * P : (c + 1) * P].bitcast(FP4X4),
                    lhsT_scale=k_scales[:, block * P : (block + 1) * P],
                    rhs=q_codes[:].bitcast(FP8X4),
                    rhs_scale=q_scales[:],
                    start=True,
                    stop=True,
                )

        by_group = [P, BANK_BLOCKS, GROUPS, GROUP]
        lam_rows = lam_turned[:].rearrange("p (o v g) -> p o v g", o=1, g=GROUP).to_broadcast(by_group)
        raw_sb = [tile([P, BANK_BLOCKS, Q], F32, f"raw_sb{b}") for b in range(SLOT_BANKS)]
        shift = [tile(by_group, F32, f"shift{b}") for b in range(SLOT_BANKS)]
        neg_best = [tile([P, BANK_BLOCKS, GROUPS, 1], F32, f"neg_best{b}") for b in range(SLOT_BANKS)]
        for b in range(SLOT_BANKS):
            nc.vector.tensor_reduce(
                neg_best[b][:].rearrange("p c v o -> p (c v o)"),
                raw[b][:].rearrange("p c (v g) -> p (c v) g", g=GROUP),
                axis=AXIS.X,
                op=ALU.max,
                negate=True,
            )
            nc.scalar.copy(raw_sb[b][:], raw[b][:])
        for b in range(SLOT_BANKS):
            nc.vector.tensor_tensor(shift[b][:], neg_best[b][:].to_broadcast(by_group), lam_rows, ALU.mult)

        score = [ps.tile([P, I], F32, name=f"score{h}", tag=f"turn{h}") for h in range(HALVES)]
        for h in range(HALVES):
            for b in range(SLOT_BANKS):
                terms = [raw_sb[b][:], shift[b][:].rearrange("p c v g -> p c (v g)")]
                for n, term in enumerate(terms):
                    for c in range(BANK_BLOCKS):
                        block = BANK_BLOCKS * b + c
                        nc.tensor.matmul(
                            score[h][:, block * P : (block + 1) * P],
                            lhsT=term[:, c, h * P : (h + 1) * P],
                            rhs=ident[:],
                            is_transpose=True,
                            start=(b == 0 and n == 0 and c == 0),
                            stop=(b == SLOT_BANKS - 1 and n == len(terms) - 1 and c == BANK_BLOCKS - 1),
                        )

        p_sb = [tile([P, I], F32, f"p{h}") for h in range(HALVES)]
        p_inv = [tile([P, I], F32, f"p_inv{h}") for h in range(HALVES)]
        ratio = [tile([P, I], F32, f"ratio{h}") for h in range(HALVES)]
        for h in range(HALVES):
            nc.scalar.activation(p_sb[h][:], score[h][:], ACT.Exp)
            nc.scalar.activation(p_inv[h][:], score[h][:], ACT.Exp, scale=-1.0)
        piece = I // 2
        for h in range(HALVES):
            for first in range(0, I, piece):
                cols = slice(first, first + piece)
                nc.vector.tensor_tensor(
                    ratio[h][:, cols],
                    p_sb[h][:].indirect(rival_list[:, first // LIST_ROWS : (first + piece) // LIST_ROWS]),
                    p_inv[h][:, cols],
                    ALU.mult,
                )

        factor_rows = ps.tile([P, PACK, P], F32, name="factor_rows", tag="factor_rows")
        for t in range(PACK):
            nc.tensor.transpose(factor_rows[:, t, :], factor_col[:, t : t + 1].to_broadcast([P, P]), ident[:])

        root = [tile([P, I], F32, f"root{h}") for h in range(HALVES)]
        part = [tile([P, I], F32, f"part{h}") for h in range(HALVES)]
        part_sum = [tile([P, 1], F32, f"part_sum{h}") for h in range(HALVES)]
        inv_sum = [tile([P, 1], F32, f"inv_sum{h}") for h in range(HALVES)]
        w_bf = [tile([P, 2, P, 2], BF16, f"w_bf{h}") for h in range(HALVES)]
        w_codes = tile([P, Q], U32, "w_codes")
        w_scales = tile([P, Q], U8, "w_scales")
        for h in range(HALVES):
            nc.scalar.activation(
                root[h][:], ratio[h][:], ACT.Abs_reciprocal_sqrt, scale=rival_col[:, h : h + 1], bias=1.0
            )
        for h in range(HALVES):
            nc.scalar.activation(part[h][:], root[h][:], ACT.Square, accum_out=part_sum[h][:])

        for h in range(HALVES):
            cols = slice(h * P, (h + 1) * P)
            nc.vector.reciprocal(inv_sum[h][:], part_sum[h][:])
            w_turned = ps.tile([P, 2, P], F32, name=f"w_turned{h}", tag=f"turn{h}")
            for u in range(2):
                nc.vector.scalar_tensor_tensor(
                    w_bf[h][:, u],
                    part[h][:].rearrange("q (p u e) -> q u p e", u=2, e=2)[:, u],
                    inv_sum[h][:],
                    factor_rows[:, 2 * u : 2 * u + 2, :].rearrange("q e p -> q p e"),
                    ALU.mult,
                    ALU.mult,
                )
                nc.tensor.transpose(
                    w_turned[:, u, :], w_bf[h][:, u].rearrange("q p e -> q (p e)").bitcast(F32), ident[:]
                )
            w_grouped = tile([P, P * PACK], BF16, f"w_grouped{h}")
            nc.vector.tensor_copy(
                w_grouped[:].bitcast(F32).rearrange("p (c u) -> p c u", u=2), w_turned[:].rearrange("p u c -> p c u")
            )
            nc.vector.quantize_mx(w_codes[:, cols].bitcast(FP8X4), w_scales[:, cols], w_grouped[:])

        v_codes = tile([P, E], U32, "v_codes")
        v_scales = tile([P, E], U8, "v_scales")

        def turn_pairs(rows_bf, turned):
            pairs = rows_bf.bitcast(F32)
            for u in range(2):
                nc.tensor.transpose(turned[:, u, :], pairs[:, u : I // 2 : 2], ident[:])

        def gather_values(j, on_scalar, reuse):
            picked = tile([P, I], BF16, f"v_picked{j}", reuse)
            if on_scalar:
                nc.scalar.activation(picked[:], val_pool[j][:].indirect(slot_list[:]), ACT.Copy)
            else:
                nc.vector.tensor_copy(picked[:], val_pool[j][:].indirect(slot_list[:]))
            return picked

        def quantize_values(first, picked, bank, copy, reuse):
            count = len(picked)
            turned = ps.tile([P, count, 2, P], F32, name=f"v_turned{first}", tag=bank)
            for n in range(count):
                turn_pairs(picked[n][:], turned[:, n])
            grouped = tile([P, count * P * PACK], BF16, f"v_grouped{first}", reuse)
            copy(
                grouped[:].bitcast(F32).rearrange("p (j c u) -> p j c u", j=count, u=2),
                turned[:].rearrange("p j u c -> p j c u"),
            )
            cols = slice(first * P, (first + count) * P)
            nc.vector.quantize_mx(v_codes[:, cols].bitcast(FP8X4), v_scales[:, cols], grouped[:])

        quantize_values(0, [gather_values(0, True, None)], "values0", nc.vector.tensor_copy, None)
        middle = [gather_values(1, True, "neg_best0"), gather_values(2, False, None)]
        quantize_values(1, middle, "values1", nc.scalar.copy, "ratio1")
        quantize_values(3, [gather_values(3, False, "p_inv1")], "values0", nc.scalar.copy, "root0")

        gain_row = tile([P, Q], F32, "gain_row", "neg_best1")
        gain_col = tile([P, HALVES], F32, "gain_col")
        gain = tile([P, Q], F32, "gain", "ratio0")
        nc.vector.tensor_copy(gain_row[:], gain_pool[:].indirect(member_list[:]))
        gain_turned = ps.tile([P, HALVES, P], F32, name="gain_turned", tag="rows")
        for h in range(HALVES):
            nc.tensor.transpose(gain_turned[:, h, :], gain_row[:, h * P : (h + 1) * P], ident[:])
        nc.vector.tensor_copy(gain_col[:], gain_turned[:, :, 0])
        gain_spread = ps.tile([P, Q], F32, name="gain_spread", tag="rows")
        for h in range(HALVES):
            nc.tensor.transpose(
                gain_spread[:, h * P : (h + 1) * P], gain_col[:, h : h + 1].to_broadcast([P, P]), ident[:]
            )
        nc.scalar.copy(gain[:], gain_spread[:])

        mem_picked = tile([P, HALVES, PACK, P], F32, "mem_picked", "root1")
        half_cols = P // LIST_ROWS
        for h in range(HALVES):
            for j in range(PACK):
                listed = mem_pool[j][:].indirect(member_list[:, half_cols * h : half_cols * (h + 1)])
                nc.scalar.activation(mem_picked[:, h, j, :], listed, ACT.Copy)
        scaled = [tile([P, PACK, P], F32, f"scaled{h}") for h in range(HALVES)]
        y = [tile([P, PACK, P], F32, f"y{h}") for h in range(HALVES)]
        y_bf = [tile([P, P, PACK], BF16, f"y_bf{h}") for h in range(HALVES)]
        y_codes = tile([P, Q], U32, "y_codes")
        y_scales = tile([P, Q], U8, "y_scales")
        out_dealt = out_0.rearrange("(p j) q -> p j q", j=PACK)
        for h in range(HALVES):
            cols = slice(h * P, (h + 1) * P)
            o = ps.tile([P, PACK, P], F32, name=f"o{h}", tag=f"product{h}")
            for j in range(PACK):
                nc.tensor.matmul_mx(
                    o[:, j, :],
                    lhsT=v_codes[:, j * P : (j + 1) * P].bitcast(FP8X4),
                    lhsT_scale=v_scales[:, j * P : (j + 1) * P],
                    rhs=w_codes[:, cols].bitcast(FP8X4),
                    rhs_scale=w_scales[:, cols],
                    start=True,
                    stop=True,
                )
            nc.vector.tensor_tensor(
                scaled[h][:],
                o[:],
                gain[:, cols].rearrange("p (o c) -> p o c", o=1).to_broadcast([P, PACK, P]),
                ALU.mult,
            )
            nc.vector.tensor_tensor(y[h][:], mem_picked[:, h], scaled[h][:], ALU.add)
            nc.sync.dma_start(out_dealt[:, :, cols], y[h][:])
            y_src = y[h][:].rearrange("p t (c i) -> p c t i", i=RUN)
            y_dst = y_bf[h][:].rearrange("p (c i) t -> p c t i", i=RUN)
            if h < HALVES - 1:
                nc.scalar.copy(y_dst, y_src)
            else:
                nc.scalar.copy(y_dst[:, :LAST_SCALAR_RUNS], y_src[:, :LAST_SCALAR_RUNS])
                nc.vector.tensor_copy(y_dst[:, LAST_SCALAR_RUNS:], y_src[:, LAST_SCALAR_RUNS:])
            nc.vector.quantize_mx(
                y_codes[:, cols].bitcast(FP8X4), y_scales[:, cols], y_bf[h][:].rearrange("p c t -> p (c t)")
            )
        nc.scalar.dma_start(out_1[0].rearrange("p c r -> p (c r)").bitcast(I32), y_codes[:].bitcast(I32))
        for quad in range(QUADRANTS):
            [nc.sync, nc.scalar][quad % 2].dma_start(
                out_2[0, 4 * quad : 4 * quad + 4, :].bitcast(I32),
                y_scales[32 * quad : 32 * quad + 4, :].bitcast(I32),
            )
